import numpy as np
import ml_dtypes


def mxq(x, axis, fmt="e4m3"):
    dtype, down = {"e4m3": (ml_dtypes.float8_e4m3fn, 7), "e5m2": (ml_dtypes.float8_e5m2, 14)}[fmt]
    v = np.moveaxis(np.asarray(x, np.float32).astype(ml_dtypes.bfloat16).astype(np.float64), axis, -1)
    blocks = v.reshape(v.shape[:-1] + (-1, 32))
    amax = np.abs(blocks).max(-1, keepdims=True)
    byte = np.maximum(np.where(amax > 0, np.frexp(amax)[1] - 1 + 127, 0) - down, 1)
    scale = np.exp2(byte - 127.0)
    codes = (blocks / scale).astype(np.float32).astype(dtype).astype(np.float64)
    return np.moveaxis((codes * scale).reshape(v.shape), -1, axis)


WIDE = False


def mx_kscale(k):
    if not WIDE:
        return np.ones(k)
    levels = np.array([10, -10, 5, -5, 0])
    if k % 512:
        return np.exp2(np.random.permutation(np.resize(levels, k // 32))).repeat(32)
    a = np.empty((k // 512, 16))
    for p in range(k // 512):
        a[p, :8] = np.random.permutation(np.resize(levels, 8))
        for g in range(8):
            far = levels[np.abs(levels - a[p, g]) >= 10]
            a[p, g + 8] = far[np.random.randint(len(far))]
    return np.exp2(a.ravel()).repeat(32)


def f64(x):
    return np.asarray(x).astype(np.float64)


def striped(idx):
    return np.tile(idx.reshape(-1, 16).T, (8, 1)).astype(np.uint16)


def unstriped(offs):
    return offs[:16].T.reshape(-1).astype(np.int64)


E2M1 = np.array([0.0, 0.5, 1.0, 1.5, 2.0, 3.0, 4.0, 6.0, -0.0, -0.5, -1.0, -1.5, -2.0, -3.0, -4.0, -6.0])


def pack_weight(w, fmt):
    k, n = w.shape
    w = f64(np.asarray(w, np.float32).astype(ml_dtypes.bfloat16)).reshape(k // 32, 32, n)
    amax = np.abs(w).max(1)
    if fmt == "e4m3":
        byte = np.frexp(amax)[1] - 1 + 127 - 7
    else:
        mant, ex = np.frexp(amax / 6.0)
        byte = np.where(mant > 0.5, ex, ex - 1) + 127
    byte = np.clip(np.where(amax > 0, byte, 1), 1, 254)
    scaled = (w * np.exp2(127.0 - byte)[:, None, :]).reshape(k, n).astype(np.float32)
    by_word = np.ascontiguousarray(scaled.reshape(k // 512, 128, 4, n).transpose(0, 1, 3, 2))
    if fmt == "e4m3":
        words = by_word.astype(ml_dtypes.float8_e4m3fn).view(np.uint8)
    else:
        c = by_word.astype(ml_dtypes.float4_e2m1fn).view(np.uint8) & 0xF
        words = (c[..., 0::2] | (c[..., 1::2] << 4)).reshape(k // 512, 128, 2 * n)
    return np.ascontiguousarray(words), np.ascontiguousarray(byte.astype(np.uint8).reshape(k // 512, 16, n))


def unpack_weight(words, scales, fmt):
    g, _, n = scales.shape
    words = np.ascontiguousarray(words).reshape(g, 128, n, -1)
    if fmt == "e4m3":
        vals = words.view(ml_dtypes.float8_e4m3fn).astype(np.float64)
    else:
        nib = np.empty((g, 128, n, 4), np.uint8)
        nib[..., 0::2] = words & 0xF
        nib[..., 1::2] = words >> 4
        vals = E2M1[nib]
    vals = vals * np.repeat(np.exp2(scales.astype(np.float64) - 127.0), 8, axis=1)[..., None]
    return vals.transpose(0, 1, 3, 2).reshape(g * 512, n)


def gelu(v):
    return 0.5 * v * (1.0 + np.tanh(np.sqrt(2.0 / np.pi) * (v + 0.044715 * v**3)))


K, K2, H, N, T, S, T2, P = 1024, 512, 1024, 512, 2048, 512, 2048, 1024

def setup_inputs():
    n = np.random.standard_normal
    s, s2, u = mx_kscale(K)[:, None], mx_kscale(K2)[:, None], mx_kscale(H)[:, None]
    d = {}
    d["tab_words"], d["tab_scales"] = pack_weight(n((K, T)) * s, "e4m3")
    d["tab2_words"], d["tab2_scales"] = pack_weight(n((K2, T)) * s2, "e4m3")
    d["offs"] = striped(np.random.permutation(T)[:S])
    d["offs2"] = striped(np.random.permutation(T)[:S])
    perm = np.random.permutation(T2)
    d["offs3"] = striped(perm[:S])
    d["offs4"] = striped(perm[S:2 * S])
    d["offs5"] = striped(np.random.permutation(T2)[:P])
    d["w1"] = (n((K, H)) / K ** 0.5 / s * u.T).astype(np.float32)
    d["w2_words"], d["w2_scales"] = pack_weight(n((K2, H)) / K2 ** 0.5 / s2, "e2m1")
    d["gain"] = (np.exp(0.4 * n(H)) * u[:, 0]).astype(np.float32)
    d["wg1"] = np.exp(0.3 * n((128, S))).astype(np.float32)
    d["wg2"] = np.exp(0.3 * n((128, S))).astype(np.float32)
    d["page0"] = (n((H, T2)) * u).astype(np.float32)
    d["cap"] = ((0.6 + 0.5 * n(H)) * u[:, 0]).astype(np.float32)
    d["wa"] = (1.6 * n((H, N)) / H ** 0.5 / u).astype(np.float32)
    d["wb_words"], d["wb_scales"] = pack_weight(n((H, N)) / H ** 0.5 / u, "e4m3")
    d["wc_words"], d["wc_scales"] = pack_weight(n((H, N)) / H ** 0.5 / u, "e2m1")
    return d

def reference(tab_words, tab_scales, tab2_words, tab2_scales, offs, offs2, offs3, offs4, offs5, w1, w2_words, w2_scales, gain, wg1, wg2, page0, cap, wa, wb_words, wb_scales, wc_words, wc_scales):
    v = unpack_weight(tab_words, tab_scales, "e4m3")[:, unstriped(offs)]
    v2 = unpack_weight(tab2_words, tab2_scales, "e4m3")[:, unstriped(offs2)]
    h1 = np.abs(mxq(f64(w1), 0, "e4m3").T @ v)
    h2 = f64(gain)[:, None] * (unpack_weight(w2_words, w2_scales, "e2m1").T @ v2)
    page = f64(page0).copy()
    page[:, unstriped(offs3)] = np.tile(f64(wg1), (H // 128, 1)) * h1
    page[:, unstriped(offs4)] = np.tile(f64(wg2), (H // 128, 1)) * h2
    x = np.minimum(page[:, unstriped(offs5)], f64(cap)[:, None])
    xq = mxq(x, 0, "e4m3")
    ya = mxq(f64(wa), 0, "e4m3").T @ xq
    yb = unpack_weight(wb_words, wb_scales, "e4m3").T @ xq
    yc = unpack_weight(wc_words, wc_scales, "e2m1").T @ xq
    return np.maximum(np.tanh(ya), yb) - yc

@@ -1,0 +1,295 @@
+from contextlib import ExitStack
+
+import concourse.mybir as mybir
+from concourse.masks import make_identity
+
+K, K2, H, N, T, S, T2, J = 1024, 512, 1024, 512, 2048, 512, 2048, 1024
+FLOPS = 2 * (K * H * S + K2 * H * S + 3 * H * N * J)
+
+F32 = mybir.dt.float32
+BF16 = mybir.dt.bfloat16
+I32 = mybir.dt.int32
+U32 = mybir.dt.uint32
+U16 = mybir.dt.uint16
+U8 = mybir.dt.uint8
+E4M3 = mybir.dt.float8_e4m3fn_x4
+E2M1 = mybir.dt.float4_e2m1fn_x4
+ALU = mybir.AluOpType
+ACT = mybir.ActivationFunctionType
+
+P = 128
+W = 512
+
+
+def tile_list_logo_conflict_register_kernel(
+    tc, tab_words, tab_scales, tab2_words, tab2_scales, offs, offs2, offs3, offs4, offs5,
+    w1, w2_words, w2_scales, gain, wg1, wg2, page0, cap, wa, wb_words, wb_scales, wc_words, wc_scales, out,
+):
+    nc = tc.nc
+    with ExitStack() as ctx:
+        sb = ctx.enter_context(tc.tile_pool(name="sb", bufs=1))
+        ps = ctx.enter_context(tc.psum_pool(name="ps", bufs=1))
+
+        def tile(name, shape, dtype, tag=None):
+            return sb.tile(shape, dtype, name=name, tag=tag or name, align_bytes=64)
+
+        def load(dst, src):
+            nc.sync.dma_start(dst, src)
+
+        def load_list(name, src):
+            lst = tile(name, list(src.shape), U16)
+            nc.sync.dma_start(lst[:], src)
+            return lst
+
+        def zeroed_plane(name, shape):
+            plane = tile(name, shape, U8)
+            nc.vector.memset(plane[:].bitcast(I32), 0)
+            return plane
+
+        banks = [ps.tile([P, W], F32, name="bank%d" % i) for i in range(8)]
+
+        w2_plane = zeroed_plane("w2_plane", [P, H])
+        tab2_plane = zeroed_plane("tab2_plane", [P, T])
+        tab_plane = zeroed_plane("tab_plane", [P, T])
+        wb_plane = zeroed_plane("wb_plane", [P, N])
+        wc_plane = zeroed_plane("wc_plane", [P, 2 * N])
+        ident = tile("ident", [P, P], F32)
+        make_identity(nc, ident[:])
+        warm = tile("warm", [P, 1], F32)
+        nc.scalar.activation(warm[:], ident[:, 0:1], ACT.Tanh)
+
+        tab2_rows = tile("tab2_rows", [P, T // 4], I32)
+        for q in range(4):
+            load(tab2_rows[32 * q : 32 * q + 4, :], tab2_scales[0, 4 * q : 4 * q + 4, :].bitcast(I32))
+        list2 = load_list("list2", offs2)
+        wg2_raw = tile("wg2_raw", [P, S], F32)
+        load(wg2_raw[:], wg2)
+        w2_raw = tile("w2_raw", [P, 2 * H], U8)
+        load(w2_raw[:].bitcast(I32), w2_words[0].bitcast(I32))
+        tab2_w = tile("tab2_w", [P, T], I32, tag="t2")
+        load(tab2_w[:], tab2_words[0].rearrange("p t i -> p (t i)").bitcast(I32))
+        for q in range(4):
+            load(w2_plane[32 * q : 32 * q + 4, :].bitcast(I32), w2_scales[0, 4 * q : 4 * q + 4, :].bitcast(I32))
+        page_rows = page0.rearrange("(b p t) c -> b t p c", b=2, t=4)
+        pages = [tile("page%d" % s, [P, T2], F32) for s in range(8)]
+        load(pages[0][:], page_rows[0, 0])
+        list4 = load_list("list4", offs4)
+        gain_sb = tile("gain_sb", [P, 2, 4], F32)
+        load(gain_sb[:], gain.rearrange("(b p t) -> p b t", b=2, t=4))
+        for s in range(1, 8):
+            load(pages[s][:], page_rows[s // 4, s % 4])
+        wg1_raw = tile("wg1_raw", [P, S], F32)
+        load(wg1_raw[:], wg1)
+        list1 = load_list("list1", offs)
+        list3 = load_list("list3", offs3)
+        list5 = load_list("list5", offs5)
+        cap_sb = tile("cap_sb", [P, 2, 4], F32)
+        load(cap_sb[:], cap.rearrange("(b p t) -> p b t", b=2, t=4))
+        for q in range(4):
+            load(tab_plane[32 * q : 32 * q + 8, :].bitcast(I32), tab_scales[:, 4 * q : 4 * q + 4, :].bitcast(I32))
+        tab_w = [tile("tab_w%d" % a, [P, T], I32, tag="t%d" % a) for a in range(2)]
+        for a in range(2):
+            load(tab_w[a][:], tab_words[a].rearrange("p t i -> p (t i)").bitcast(I32))
+        w1_rows = w1.rearrange("(a p j) (b c) -> b a p j c", a=2, j=4, b=2)
+        w1_raw = [[tile("w1_raw%d%d" % (b, a), [P, 4, W], F32, tag="r%d%d" % (b, a)) for a in range(2)] for b in range(2)]
+        for b in range(2):
+            for a in range(2):
+                load(w1_raw[b][a][:], w1_rows[b, a])
+        for q in range(4):
+            load(wb_plane[32 * q : 32 * q + 8, :].bitcast(I32), wb_scales[:, 4 * q : 4 * q + 4, :].bitcast(I32))
+        for q in range(4):
+            load(
+                wc_plane[32 * q : 32 * q + 4, :].bitcast(I32).rearrange("p (a n) -> p a n", a=2),
+                wc_scales[:, 4 * q : 4 * q + 4, :].bitcast(I32).rearrange("a r n -> r a n"),
+            )
+        wb_w = tile("wb_w", [P, 2, N], I32)
+        load(wb_w[:], wb_words.rearrange("a p n i -> p a (n i)").bitcast(I32))
+        wc_w = tile("wc_w", [P, 2, 2 * N], U8)
+        load(wc_w[:].bitcast(I32), wc_words.rearrange("a p c -> p a c").bitcast(I32))
+
+        w2_c = tile("w2_c", [P, 2 * H], U8)
+        w2_s = tile("w2_s", [P, H], U8)
+        v2_c = tile("v2_c", [P, S], U32)
+        v2_s = tile("v2_s", [P, S], U8)
+
+        def deal_w2_words(b):
+            nc.vector.tensor_copy(
+                w2_c[:, 1024 * b : 1024 * (b + 1)].bitcast(U16).rearrange("p (t q) -> p t q", t=4),
+                w2_raw[:, 1024 * b : 1024 * (b + 1)].bitcast(U16).rearrange("p (q t) -> p t q", t=4),
+            )
+
+        def deal_w2_scales(b):
+            nc.vector.tensor_copy(
+                w2_s[:, W * b : W * (b + 1)].rearrange("p (t q) -> p t q", t=4),
+                w2_plane[:, W * b : W * (b + 1)].rearrange("p (q t) -> p t q", t=4),
+            )
+
+        def place_rows(plane, rows):
+            for q in range(4):
+                nc.vector.tensor_copy(plane[32 * q : 32 * q + 4, :].bitcast(I32), rows[32 * q : 32 * q + 4, :])
+
+        place_rows(tab2_plane, tab2_rows)
+        nc.vector.tensor_copy(v2_s[:], tab2_plane[:].indirect(list2[:]))
+        deal_w2_words(0)
+        deal_w2_words(1)
+        nc.vector.tensor_copy(v2_c[:], tab2_w[:].bitcast(U32).indirect(list2[:]))
+        deal_w2_scales(0)
+        deal_w2_scales(1)
+
+        spread = [tile("spread%d" % i, [P, S], F32) for i in range(2)]
+
+        def turn_factors(raw):
+            for c in range(4):
+                nc.tensor.transpose(banks[0][:, P * c : P * (c + 1)], raw[:, P * c : P * (c + 1)], ident[:])
+
+        def deal_factors(name, t, bank):
+            buf = spread[t % 2]
+            picked = banks[0][:].rearrange("p (c q t) -> p t c q", c=4, t=4)[:, t]
+            nc.scalar.copy(
+                buf[:].rearrange("p (c u q) -> p c u q", c=4, u=4),
+                picked.unsqueeze(2).broadcast_to([P, 4, 4, 32]),
+            )
+            for c in range(4):
+                nc.tensor.transpose(bank[:, P * c : P * (c + 1)], buf[:, P * c : P * (c + 1)], ident[:])
+            dealt = tile("%s_%d" % (name, t), [P, S], F32)
+            nc.scalar.copy(dealt[:], bank[:])
+            return dealt
+
+        hbuf = [tile("h%d" % i, [P, S], F32) for i in range(4)]
+
+        turn_factors(wg2_raw)
+        f2 = []
+        for s in range(8):
+            b, t = divmod(s, 4)
+            if b == 0:
+                f2.append(deal_factors("f2", t, banks[2 + t]))
+            bank = banks[3 + s % 3]
+            nc.tensor.matmul_mx(
+                out=bank[:], lhsT=w2_c[:, 256 * s : 256 * (s + 1)].bitcast(E2M1), lhsT_scale=w2_s[:, P * s : P * (s + 1)],
+                rhs=v2_c[:].bitcast(E4M3), rhs_scale=v2_s[:], start=True, stop=True,
+            )
+            nc.scalar.activation(hbuf[s % 4][:], bank[:], ACT.Copy, scale=gain_sb[:, b, t : t + 1])
+            nc.vector.tensor_tensor(pages[s][:].indirect(list4[:]), hbuf[s % 4][:], f2[t][:], ALU.mult)
+
+        turn_factors(wg1_raw)
+        f1 = [deal_factors("f1", t, banks[1 + t % 2]) for t in range(4)]
+        v_c = [tile("v_c%d" % a, [P, S], U32) for a in range(2)]
+        v_s = tile("v_s", [P, S], U8)
+        nc.vector.tensor_copy(v_s[:], tab_plane[:].indirect(list1[:]))
+        for a in range(2):
+            nc.vector.tensor_copy(v_c[a][:], tab_w[a][:].bitcast(U32).indirect(list1[:]))
+
+        wa_rows = wa.rearrange("(a p j) n -> a p j n", a=2, j=4)
+        wa_raw = [tile("wa_raw%d" % a, [P, 4, N], F32, tag="t%d" % a) for a in range(2)]
+        for a in range(2):
+            load(wa_raw[a][:], wa_rows[a])
+
+        stage = [tile("stage%d" % b, [P, 4 * W], F32) for b in range(2)]
+        w1_c = [tile("w1_c%d" % b, [P, 1024], U32) for b in range(2)]
+        w1_s = [tile("w1_s%d" % b, [P, 1024], U8) for b in range(2)]
+
+        def quantise_w1(b):
+            grouped = stage[b][:].bitcast(BF16).rearrange("p (t a m j) -> p a m j t", t=4, a=2, j=4)
+            for a in range(2):
+                nc.scalar.copy(grouped[:, a], w1_raw[b][a][:].rearrange("p j (m t) -> p m j t", t=4))
+            nc.vector.quantize_mx(w1_c[b][:].bitcast(E4M3), w1_s[b][:], stage[b][:].bitcast(BF16))
+
+        quantise_w1(0)
+        quantise_w1(1)
+
+        xb = [tile("xb0", [P, 2, 4, W], BF16), None]
+
+        def read_page(c, s, buf):
+            b, t = divmod(s, 4)
+            nc.vector.tensor_copy(buf, pages[s][:].indirect(list5[:, 32 * c : 32 * (c + 1)]))
+            nc.vector.tensor_scalar(xb[c][:, b, t, :], buf, cap_sb[:, b, t : t + 1], None, ALU.min)
+
+        def quarter(i, k):
+            return stage[i][:, W * k : W * (k + 1)]
+
+        wa_c = tile("wa_c", [P, 2 * N], U32)
+        wa_s = tile("wa_s", [P, 2 * N], U8)
+
+        def quantise_wa():
+            grouped = stage[0][:].bitcast(BF16).rearrange("p (a c i j) -> p a c j i", a=2, i=4, j=4)
+            for a in range(2):
+                nc.scalar.copy(grouped[:, a], wa_raw[a][:].rearrange("p j (c i) -> p c j i", i=4))
+            nc.vector.quantize_mx(wa_c[:].bitcast(E4M3), wa_s[:], stage[0][:].bitcast(BF16))
+
+        x_c = [[tile("x_c%d%d" % (c, a), [P, W], U32) for a in range(2)] for c in range(2)]
+        x_s = [[tile("x_s%d%d" % (c, a), [P, W], U8) for a in range(2)] for c in range(2)]
+        woven = tile("woven", [P, 4 * W], BF16)
+
+        def quantise_x(c, a, grouped):
+            nc.scalar.copy(
+                grouped.rearrange("p (c i t) -> p c t i", i=4, t=4),
+                xb[c][:, a].rearrange("p t (c i) -> p c t i", i=4),
+            )
+            nc.vector.quantize_mx(x_c[c][a][:].bitcast(E4M3), x_s[c][a][:], grouped)
+
+        def put_h1(s):
+            b, t = divmod(s, 4)
+            bank = banks[3 + (s + 2) % 3]
+            for a in range(2):
+                cols = slice(256 * t + P * a, 256 * t + P * (a + 1))
+                nc.tensor.matmul_mx(
+                    out=bank[:], lhsT=w1_c[b][:, cols].bitcast(E4M3), lhsT_scale=w1_s[b][:, cols],
+                    rhs=v_c[a][:].bitcast(E4M3), rhs_scale=v_s[4 * a :, :], start=(a == 0), stop=(a == 1),
+                )
+            nc.scalar.activation(hbuf[s % 4][:], bank[:], ACT.Abs)
+            nc.vector.tensor_tensor(pages[s][:].indirect(list3[:]), hbuf[s % 4][:], f1[t][:], ALU.mult)
+
+        for s in range(7):
+            put_h1(s)
+            read_page(0, s, quarter(0, s) if s < 2 else quarter(1, (s - 2) % 4))
+        put_h1(7)
+        quantise_wa()
+        quantise_x(0, 0, woven[:])
+        read_page(0, 7, quarter(0, 0))
+        half = [stage[1][:, 2 * W * i : 2 * W * (i + 1)].bitcast(BF16) for i in range(2)]
+        quantise_x(0, 1, half[0])
+        xb[1] = tile("xb1", [P, 2, 4, W], BF16, tag="t2")
+        read_page(1, 7, quarter(0, 1))
+        read_page(1, 4, quarter(0, 0))
+        read_page(1, 5, quarter(1, 0))
+        read_page(1, 6, quarter(1, 1))
+        quantise_x(1, 1, woven[:])
+        for s in range(4):
+            read_page(1, s, quarter(1, s % 2))
+        quantise_x(1, 0, half[1])
+
+        bounded = tile("bounded", [P, 4, W], F32, tag="r00")
+        offset = tile("offset", [P, 4, W], F32, tag="r01")
+        scores = [tile("scores%d" % c, [P, 4, W], F32, tag="r1%d" % c) for c in range(2)]
+
+        def product(bank, c, n, codes, plane):
+            order = (0, 1) if c == 0 else (1, 0)
+            for a in order:
+                nc.tensor.matmul_mx(
+                    out=bank[:], lhsT=codes(a, n), lhsT_scale=plane(a, n),
+                    rhs=x_c[c][a][:].bitcast(E4M3), rhs_scale=x_s[c][a][:], start=(a == order[0]), stop=(a == order[1]),
+                )
+
+        for c in range(2):
+            for n in range(4):
+                ya, yc, yb = banks[n % 2], banks[2 + n % 2], banks[4 + n]
+                product(ya, c, n, lambda a, n: wa_c[:, N * a + P * n : N * a + P * (n + 1)].bitcast(E4M3),
+                        lambda a, n: wa_s[:, N * a + P * n : N * a + P * (n + 1)])
+                product(yb, c, n, lambda a, n: wb_w[:, a, P * n : P * (n + 1)].bitcast(E4M3),
+                        lambda a, n: wb_plane[4 * a :, P * n : P * (n + 1)])
+                product(yc, c, n, lambda a, n: wc_w[:, a, 256 * n : 256 * (n + 1)].bitcast(E2M1),
+                        lambda a, n: wc_plane[:, N * a + P * n : N * a + P * (n + 1)])
+                nc.scalar.activation(bounded[:, n, :], ya[:], ACT.Tanh)
+                larger = quarter(1, n % 2)
+                nc.vector.tensor_tensor(larger, bounded[:, n, :], yb[:], ALU.max)
+                rows = slice(P * n, P * (n + 1))
+                if c == 0:
+                    nc.scalar.copy(offset[:, n, :], yc[:])
+                    nc.vector.tensor_tensor(scores[c][:, n, :], larger, offset[:, n, :], ALU.subtract)
+                    nc.sync.dma_start(out[rows, 0:W], scores[c][:, n, :])
+                else:
+                    pieces = 2 if n == 3 else 1
+                    for i in range(pieces):
+                        cols = slice(W // pieces * i, W // pieces * (i + 1))
+                        nc.vector.tensor_tensor(scores[c][:, n, cols], larger[:, cols], yc[:, cols], ALU.subtract)
+                        nc.sync.dma_start(out[rows, W + cols.start : W + cols.stop], scores[c][:, n, cols])

@@ -64,10 +64,10 @@ def tile_list_logo_conflict_register_kernel(
         list2 = load_list("list2", offs2)
         wg2_raw = tile("wg2_raw", [P, S], F32)
         load(wg2_raw[:], wg2)
-        w2_raw = tile("w2_raw", [P, 2 * H], U8)
-        load(w2_raw[:].bitcast(I32), w2_words[0].bitcast(I32))
         tab2_w = tile("tab2_w", [P, T], I32, tag="t2")
         load(tab2_w[:], tab2_words[0].rearrange("p t i -> p (t i)").bitcast(I32))
+        w2_raw = tile("w2_raw", [P, 2 * H], U8)
+        load(w2_raw[:].bitcast(I32), w2_words[0].bitcast(I32))
         for q in range(4):
             load(w2_plane[32 * q : 32 * q + 4, :].bitcast(I32), w2_scales[0, 4 * q : 4 * q + 4, :].bitcast(I32))
         page_rows = page0.rearrange("(b p t) c -> b t p c", b=2, t=4)
@@ -76,12 +76,11 @@ def tile_list_logo_conflict_register_kernel(
         list4 = load_list("list4", offs4)
         gain_sb = tile("gain_sb", [P, 2, 4], F32)
         load(gain_sb[:], gain.rearrange("(b p t) -> p b t", b=2, t=4))
-        for s in range(1, 8):
+        for s in range(1, 7):
             load(pages[s][:], page_rows[s // 4, s % 4])
         wg1_raw = tile("wg1_raw", [P, S], F32)
         load(wg1_raw[:], wg1)
         list1 = load_list("list1", offs)
-        list3 = load_list("list3", offs3)
         list5 = load_list("list5", offs5)
         cap_sb = tile("cap_sb", [P, 2, 4], F32)
         load(cap_sb[:], cap.rearrange("(b p t) -> p b t", b=2, t=4))
@@ -95,6 +94,9 @@ def tile_list_logo_conflict_register_kernel(
         for b in range(2):
             for a in range(2):
                 load(w1_raw[b][a][:], w1_rows[b, a])
+                if (b, a) == (1, 0):
+                    load(pages[7][:], page_rows[1, 3])
+        list3 = load_list("list3", offs3)
         for q in range(4):
             load(wb_plane[32 * q : 32 * q + 8, :].bitcast(I32), wb_scales[:, 4 * q : 4 * q + 4, :].bitcast(I32))
         for q in range(4):
@@ -130,11 +132,10 @@ def tile_list_logo_conflict_register_kernel(
 
         place_rows(tab2_plane, tab2_rows)
         nc.vector.tensor_copy(v2_s[:], tab2_plane[:].indirect(list2[:]))
-        deal_w2_words(0)
-        deal_w2_words(1)
         nc.vector.tensor_copy(v2_c[:], tab2_w[:].bitcast(U32).indirect(list2[:]))
-        deal_w2_scales(0)
-        deal_w2_scales(1)
+        for b in range(2):
+            deal_w2_words(b)
+            deal_w2_scales(b)
 
         spread = [tile("spread%d" % i, [P, S], F32) for i in range(2)]
 
@@ -200,8 +201,10 @@ def tile_list_logo_conflict_register_kernel(
         xb = [tile("xb0", [P, 2, 4, W], BF16), None]
 
         def read_page(c, s, buf):
-            b, t = divmod(s, 4)
             nc.vector.tensor_copy(buf, pages[s][:].indirect(list5[:, 32 * c : 32 * (c + 1)]))
+
+        def apply_cap(c, s, buf):
+            b, t = divmod(s, 4)
             nc.vector.tensor_scalar(xb[c][:, b, t, :], buf, cap_sb[:, b, t : t + 1], None, ALU.min)
 
         def quarter(i, k):
@@ -216,7 +219,7 @@ def tile_list_logo_conflict_register_kernel(
                 nc.scalar.copy(grouped[:, a], wa_raw[a][:].rearrange("p j (c i) -> p c j i", i=4))
             nc.vector.quantize_mx(wa_c[:].bitcast(E4M3), wa_s[:], stage[0][:].bitcast(BF16))
 
-        x_c = [[tile("x_c%d%d" % (c, a), [P, W], U32) for a in range(2)] for c in range(2)]
+        x_c = [[tile("x_c%d%d" % (c, a), [P, W], U32, tag="x%d%d" % (c, a)) for a in range(2)] for c in range(2)]
         x_s = [[tile("x_s%d%d" % (c, a), [P, W], U8) for a in range(2)] for c in range(2)]
         woven = tile("woven", [P, 4 * W], BF16)
 
@@ -239,24 +242,28 @@ def tile_list_logo_conflict_register_kernel(
             nc.scalar.activation(hbuf[s % 4][:], bank[:], ACT.Abs)
             nc.vector.tensor_tensor(pages[s][:].indirect(list3[:]), hbuf[s % 4][:], f1[t][:], ALU.mult)
 
-        for s in range(7):
+        picked = [quarter(0, 0), quarter(0, 1)] + [quarter(1, s % 4) for s in range(5)] + [quarter(0, 0)]
+        for s in range(8):
             put_h1(s)
-            read_page(0, s, quarter(0, s) if s < 2 else quarter(1, (s - 2) % 4))
-        put_h1(7)
+            if s >= 1:
+                read_page(0, s - 1, picked[s - 1])
+            if s >= 2:
+                apply_cap(0, s - 2, picked[s - 2])
         quantise_wa()
         quantise_x(0, 0, woven[:])
-        read_page(0, 7, quarter(0, 0))
-        half = [stage[1][:, 2 * W * i : 2 * W * (i + 1)].bitcast(BF16) for i in range(2)]
-        quantise_x(0, 1, half[0])
+        read_page(0, 7, picked[7])
+        apply_cap(0, 6, picked[6])
+        apply_cap(0, 7, picked[7])
+        half = stage[1][:, 0 : 2 * W].bitcast(BF16)
+        quantise_x(0, 1, half)
         xb[1] = tile("xb1", [P, 2, 4, W], BF16, tag="t2")
-        read_page(1, 7, quarter(0, 1))
-        read_page(1, 4, quarter(0, 0))
-        read_page(1, 5, quarter(1, 0))
-        read_page(1, 6, quarter(1, 1))
+        for s, buf in ((7, quarter(0, 1)), (4, quarter(0, 0)), (5, quarter(1, 0)), (6, quarter(1, 1))):
+            read_page(1, s, buf)
+            apply_cap(1, s, buf)
         quantise_x(1, 1, woven[:])
         for s in range(4):
             read_page(1, s, quarter(1, s % 2))
-        quantise_x(1, 0, half[1])
+            apply_cap(1, s, quarter(1, s % 2))
 
         bounded = tile("bounded", [P, 4, W], F32, tag="r00")
         offset = tile("offset", [P, 4, W], F32, tag="r01")
@@ -270,26 +277,36 @@ def tile_list_logo_conflict_register_kernel(
                     rhs=x_c[c][a][:].bitcast(E4M3), rhs_scale=x_s[c][a][:], start=(a == order[0]), stop=(a == order[1]),
                 )
 
-        for c in range(2):
-            for n in range(4):
-                ya, yc, yb = banks[n % 2], banks[2 + n % 2], banks[4 + n]
-                product(ya, c, n, lambda a, n: wa_c[:, N * a + P * n : N * a + P * (n + 1)].bitcast(E4M3),
-                        lambda a, n: wa_s[:, N * a + P * n : N * a + P * (n + 1)])
-                product(yb, c, n, lambda a, n: wb_w[:, a, P * n : P * (n + 1)].bitcast(E4M3),
-                        lambda a, n: wb_plane[4 * a :, P * n : P * (n + 1)])
-                product(yc, c, n, lambda a, n: wc_w[:, a, 256 * n : 256 * (n + 1)].bitcast(E2M1),
-                        lambda a, n: wc_plane[:, N * a + P * n : N * a + P * (n + 1)])
-                nc.scalar.activation(bounded[:, n, :], ya[:], ACT.Tanh)
-                larger = quarter(1, n % 2)
-                nc.vector.tensor_tensor(larger, bounded[:, n, :], yb[:], ALU.max)
-                rows = slice(P * n, P * (n + 1))
-                if c == 0:
-                    nc.scalar.copy(offset[:, n, :], yc[:])
-                    nc.vector.tensor_tensor(scores[c][:, n, :], larger, offset[:, n, :], ALU.subtract)
-                    nc.sync.dma_start(out[rows, 0:W], scores[c][:, n, :])
-                else:
-                    pieces = 2 if n == 3 else 1
-                    for i in range(pieces):
-                        cols = slice(W // pieces * i, W // pieces * (i + 1))
-                        nc.vector.tensor_tensor(scores[c][:, n, cols], larger[:, cols], yc[:, cols], ALU.subtract)
-                        nc.sync.dma_start(out[rows, W + cols.start : W + cols.stop], scores[c][:, n, cols])
+        def multiply(c, n):
+            ya, yc, yb = banks[n % 2], banks[2 + n % 2], banks[4 + n]
+            product(ya, c, n, lambda a, n: wa_c[:, N * a + P * n : N * a + P * (n + 1)].bitcast(E4M3),
+                    lambda a, n: wa_s[:, N * a + P * n : N * a + P * (n + 1)])
+            product(yb, c, n, lambda a, n: wb_w[:, a, P * n : P * (n + 1)].bitcast(E4M3),
+                    lambda a, n: wb_plane[4 * a :, P * n : P * (n + 1)])
+            product(yc, c, n, lambda a, n: wc_w[:, a, 256 * n : 256 * (n + 1)].bitcast(E2M1),
+                    lambda a, n: wc_plane[:, N * a + P * n : N * a + P * (n + 1)])
+            nc.scalar.activation(bounded[:, n, :], ya[:], ACT.Tanh)
+            if c == 0:
+                nc.scalar.copy(offset[:, n, :], yc[:])
+
+        def score(c, n):
+            larger = woven_last[:, W * (n - 2) : W * (n - 1)] if c == 0 and n >= 2 else quarter(1, n % 2)
+            nc.vector.tensor_tensor(larger, bounded[:, n, :], banks[4 + n][:], ALU.max)
+            taken = offset[:, n, :] if c == 0 else banks[2 + n % 2][:]
+            pieces = 2 if (c, n) == (1, 3) else 1
+            for i in range(pieces):
+                cols = slice(W // pieces * i, W // pieces * (i + 1))
+                nc.vector.tensor_tensor(scores[c][:, n, cols], larger[:, cols], taken[:, cols], ALU.subtract)
+                nc.sync.dma_start(
+                    out[P * n : P * (n + 1), W * c + cols.start : W * c + cols.stop], scores[c][:, n, cols]
+                )
+
+        for n in range(4):
+            multiply(0, n)
+        woven_last = tile("woven_last", [P, 2 * W], F32, tag="x00")
+        quantise_x(1, 0, woven_last[:].bitcast(BF16))
+        for n in range(4):
+            score(0, n)
+        for n in range(4):
+            multiply(1, n)
+            score(1, n)

@@ -55,8 +55,6 @@ def tile_list_logo_conflict_register_kernel(
         wc_plane = zeroed_plane("wc_plane", [P, 2 * N])
         ident = tile("ident", [P, P], F32)
         make_identity(nc, ident[:])
-        warm = tile("warm", [P, 1], F32)
-        nc.scalar.activation(warm[:], ident[:, 0:1], ACT.Tanh)
 
         tab2_rows = tile("tab2_rows", [P, T // 4], I32)
         for q in range(4):
@@ -68,27 +66,28 @@ def tile_list_logo_conflict_register_kernel(
         load(tab2_w[:], tab2_words[0].rearrange("p t i -> p (t i)").bitcast(I32))
         w2_raw = tile("w2_raw", [P, 2 * H], U8)
         load(w2_raw[:].bitcast(I32), w2_words[0].bitcast(I32))
+        gain_sb = tile("gain_sb", [P, 2, 4], F32)
+        load(gain_sb[:], gain.rearrange("(b p t) -> p b t", b=2, t=4))
         for q in range(4):
             load(w2_plane[32 * q : 32 * q + 4, :].bitcast(I32), w2_scales[0, 4 * q : 4 * q + 4, :].bitcast(I32))
         page_rows = page0.rearrange("(b p t) c -> b t p c", b=2, t=4)
         pages = [tile("page%d" % s, [P, T2], F32) for s in range(8)]
         load(pages[0][:], page_rows[0, 0])
         list4 = load_list("list4", offs4)
-        gain_sb = tile("gain_sb", [P, 2, 4], F32)
-        load(gain_sb[:], gain.rearrange("(b p t) -> p b t", b=2, t=4))
-        for s in range(1, 7):
-            load(pages[s][:], page_rows[s // 4, s % 4])
+        load(pages[1][:], page_rows[0, 1])
+        load(pages[2][:], page_rows[0, 2])
+        for q in range(4):
+            load(tab_plane[32 * q : 32 * q + 8, :].bitcast(I32), tab_scales[:, 4 * q : 4 * q + 4, :].bitcast(I32))
+            load(pages[3 + q][:], page_rows[(3 + q) // 4, (3 + q) % 4])
         wg1_raw = tile("wg1_raw", [P, S], F32)
         load(wg1_raw[:], wg1)
         list1 = load_list("list1", offs)
-        list5 = load_list("list5", offs5)
-        cap_sb = tile("cap_sb", [P, 2, 4], F32)
-        load(cap_sb[:], cap.rearrange("(b p t) -> p b t", b=2, t=4))
-        for q in range(4):
-            load(tab_plane[32 * q : 32 * q + 8, :].bitcast(I32), tab_scales[:, 4 * q : 4 * q + 4, :].bitcast(I32))
         tab_w = [tile("tab_w%d" % a, [P, T], I32, tag="t%d" % a) for a in range(2)]
         for a in range(2):
             load(tab_w[a][:], tab_words[a].rearrange("p t i -> p (t i)").bitcast(I32))
+        list5 = load_list("list5", offs5)
+        cap_sb = tile("cap_sb", [P, 2, 4], F32)
+        load(cap_sb[:], cap.rearrange("(b p t) -> p b t", b=2, t=4))
         w1_rows = w1.rearrange("(a p j) (b c) -> b a p j c", a=2, j=4, b=2)
         w1_raw = [[tile("w1_raw%d%d" % (b, a), [P, 4, W], F32, tag="r%d%d" % (b, a)) for a in range(2)] for b in range(2)]
         for b in range(2):

from contextlib import ExitStack

import concourse.mybir as mybir
from concourse.masks import make_identity

K, K2, H, N, T, S, T2, J = 1024, 512, 1024, 512, 2048, 512, 2048, 1024
FLOPS = 2 * (K * H * S + K2 * H * S + 3 * H * N * J)

F32 = mybir.dt.float32
BF16 = mybir.dt.bfloat16
I32 = mybir.dt.int32
U32 = mybir.dt.uint32
U16 = mybir.dt.uint16
U8 = mybir.dt.uint8
E4M3 = mybir.dt.float8_e4m3fn_x4
E2M1 = mybir.dt.float4_e2m1fn_x4
ALU = mybir.AluOpType
ACT = mybir.ActivationFunctionType

P = 128
W = 512


def tile_list_logo_conflict_register_kernel(
    tc, tab_words, tab_scales, tab2_words, tab2_scales, offs, offs2, offs3, offs4, offs5,
    w1, w2_words, w2_scales, gain, wg1, wg2, page0, cap, wa, wb_words, wb_scales, wc_words, wc_scales, out,
):
    nc = tc.nc
    with ExitStack() as ctx:
        sb = ctx.enter_context(tc.tile_pool(name="sb", bufs=1))
        ps = ctx.enter_context(tc.psum_pool(name="ps", bufs=1))

        def tile(name, shape, dtype, tag=None):
            return sb.tile(shape, dtype, name=name, tag=tag or name, align_bytes=64)

        def load(dst, src):
            nc.sync.dma_start(dst, src)

        def load_list(name, src):
            lst = tile(name, list(src.shape), U16)
            nc.sync.dma_start(lst[:], src)
            return lst

        def zeroed_plane(name, shape):
            plane = tile(name, shape, U8)
            nc.vector.memset(plane[:].bitcast(I32), 0)
            return plane

        banks = [ps.tile([P, W], F32, name="bank%d" % i) for i in range(8)]

        w2_plane = zeroed_plane("w2_plane", [P, H])
        tab2_plane = zeroed_plane("tab2_plane", [P, T])
        tab_plane = zeroed_plane("tab_plane", [P, T])
        wb_plane = zeroed_plane("wb_plane", [P, N])
        wc_plane = zeroed_plane("wc_plane", [P, 2 * N])
        ident = tile("ident", [P, P], F32)
        make_identity(nc, ident[:])

        tab2_rows = tile("tab2_rows", [P, T // 4], I32)
        for q in range(4):
            load(tab2_rows[32 * q : 32 * q + 4, :], tab2_scales[0, 4 * q : 4 * q + 4, :].bitcast(I32))
        list2 = load_list("list2", offs2)
        wg2_raw = tile("wg2_raw", [P, S], F32)
        load(wg2_raw[:], wg2)
        tab2_w = tile("tab2_w", [P, T], I32, tag="t2")
        load(tab2_w[:], tab2_words[0].rearrange("p t i -> p (t i)").bitcast(I32))
        w2_raw = tile("w2_raw", [P, 2 * H], U8)
        load(w2_raw[:].bitcast(I32), w2_words[0].bitcast(I32))
        gain_sb = tile("gain_sb", [P, 2, 4], F32)
        load(gain_sb[:], gain.rearrange("(b p t) -> p b t", b=2, t=4))
        for q in range(4):
            load(w2_plane[32 * q : 32 * q + 4, :].bitcast(I32), w2_scales[0, 4 * q : 4 * q + 4, :].bitcast(I32))
        page_rows = page0.rearrange("(b p t) c -> b t p c", b=2, t=4)
        pages = [tile("page%d" % s, [P, T2], F32) for s in range(8)]
        load(pages[0][:], page_rows[0, 0])
        list4 = load_list("list4", offs4)
        load(pages[1][:], page_rows[0, 1])
        load(pages[2][:], page_rows[0, 2])
        for q in range(4):
            load(tab_plane[32 * q : 32 * q + 8, :].bitcast(I32), tab_scales[:, 4 * q : 4 * q + 4, :].bitcast(I32))
            load(pages[3 + q][:], page_rows[(3 + q) // 4, (3 + q) % 4])
        wg1_raw = tile("wg1_raw", [P, S], F32)
        load(wg1_raw[:], wg1)
        list1 = load_list("list1", offs)
        tab_w = [tile("tab_w%d" % a, [P, T], I32, tag="t%d" % a) for a in range(2)]
        for a in range(2):
            load(tab_w[a][:], tab_words[a].rearrange("p t i -> p (t i)").bitcast(I32))
        list5 = load_list("list5", offs5)
        cap_sb = tile("cap_sb", [P, 2, 4], F32)
        load(cap_sb[:], cap.rearrange("(b p t) -> p b t", b=2, t=4))
        w1_rows = w1.rearrange("(a p j) (b c) -> b a p j c", a=2, j=4, b=2)
        w1_raw = [[tile("w1_raw%d%d" % (b, a), [P, 4, W], F32, tag="r%d%d" % (b, a)) for a in range(2)] for b in range(2)]
        for b in range(2):
            for a in range(2):
                load(w1_raw[b][a][:], w1_rows[b, a])
                if (b, a) == (1, 0):
                    load(pages[7][:], page_rows[1, 3])
        list3 = load_list("list3", offs3)
        for q in range(4):
            load(wb_plane[32 * q : 32 * q + 8, :].bitcast(I32), wb_scales[:, 4 * q : 4 * q + 4, :].bitcast(I32))
        for q in range(4):
            load(
                wc_plane[32 * q : 32 * q + 4, :].bitcast(I32).rearrange("p (a n) -> p a n", a=2),
                wc_scales[:, 4 * q : 4 * q + 4, :].bitcast(I32).rearrange("a r n -> r a n"),
            )
        wb_w = tile("wb_w", [P, 2, N], I32)
        load(wb_w[:], wb_words.rearrange("a p n i -> p a (n i)").bitcast(I32))
        wc_w = tile("wc_w", [P, 2, 2 * N], U8)
        load(wc_w[:].bitcast(I32), wc_words.rearrange("a p c -> p a c").bitcast(I32))

        w2_c = tile("w2_c", [P, 2 * H], U8)
        w2_s = tile("w2_s", [P, H], U8)
        v2_c = tile("v2_c", [P, S], U32)
        v2_s = tile("v2_s", [P, S], U8)

        def deal_w2_words(b):
            nc.vector.tensor_copy(
                w2_c[:, 1024 * b : 1024 * (b + 1)].bitcast(U16).rearrange("p (t q) -> p t q", t=4),
                w2_raw[:, 1024 * b : 1024 * (b + 1)].bitcast(U16).rearrange("p (q t) -> p t q", t=4),
            )

        def deal_w2_scales(b):
            nc.vector.tensor_copy(
                w2_s[:, W * b : W * (b + 1)].rearrange("p (t q) -> p t q", t=4),
                w2_plane[:, W * b : W * (b + 1)].rearrange("p (q t) -> p t q", t=4),
            )

        def place_rows(plane, rows):
            for q in range(4):
                nc.vector.tensor_copy(plane[32 * q : 32 * q + 4, :].bitcast(I32), rows[32 * q : 32 * q + 4, :])

        place_rows(tab2_plane, tab2_rows)
        nc.vector.tensor_copy(v2_s[:], tab2_plane[:].indirect(list2[:]))
        nc.vector.tensor_copy(v2_c[:], tab2_w[:].bitcast(U32).indirect(list2[:]))
        for b in range(2):
            deal_w2_words(b)
            deal_w2_scales(b)

        spread = [tile("spread%d" % i, [P, S], F32) for i in range(2)]

        def turn_factors(raw):
            for c in range(4):
                nc.tensor.transpose(banks[0][:, P * c : P * (c + 1)], raw[:, P * c : P * (c + 1)], ident[:])

        def deal_factors(name, t, bank):
            buf = spread[t % 2]
            picked = banks[0][:].rearrange("p (c q t) -> p t c q", c=4, t=4)[:, t]
            nc.scalar.copy(
                buf[:].rearrange("p (c u q) -> p c u q", c=4, u=4),
                picked.unsqueeze(2).broadcast_to([P, 4, 4, 32]),
            )
            for c in range(4):
                nc.tensor.transpose(bank[:, P * c : P * (c + 1)], buf[:, P * c : P * (c + 1)], ident[:])
            dealt = tile("%s_%d" % (name, t), [P, S], F32)
            nc.scalar.copy(dealt[:], bank[:])
            return dealt

        hbuf = [tile("h%d" % i, [P, S], F32) for i in range(4)]

        turn_factors(wg2_raw)
        f2 = []
        for s in range(8):
            b, t = divmod(s, 4)
            if b == 0:
                f2.append(deal_factors("f2", t, banks[2 + t]))
            bank = banks[3 + s % 3]
            nc.tensor.matmul_mx(
                out=bank[:], lhsT=w2_c[:, 256 * s : 256 * (s + 1)].bitcast(E2M1), lhsT_scale=w2_s[:, P * s : P * (s + 1)],
                rhs=v2_c[:].bitcast(E4M3), rhs_scale=v2_s[:], start=True, stop=True,
            )
            nc.scalar.activation(hbuf[s % 4][:], bank[:], ACT.Copy, scale=gain_sb[:, b, t : t + 1])
            nc.vector.tensor_tensor(pages[s][:].indirect(list4[:]), hbuf[s % 4][:], f2[t][:], ALU.mult)

        turn_factors(wg1_raw)
        f1 = [deal_factors("f1", t, banks[1 + t % 2]) for t in range(4)]
        v_c = [tile("v_c%d" % a, [P, S], U32) for a in range(2)]
        v_s = tile("v_s", [P, S], U8)
        nc.vector.tensor_copy(v_s[:], tab_plane[:].indirect(list1[:]))
        for a in range(2):
            nc.vector.tensor_copy(v_c[a][:], tab_w[a][:].bitcast(U32).indirect(list1[:]))

        wa_rows = wa.rearrange("(a p j) n -> a p j n", a=2, j=4)
        wa_raw = [tile("wa_raw%d" % a, [P, 4, N], F32, tag="t%d" % a) for a in range(2)]
        for a in range(2):
            load(wa_raw[a][:], wa_rows[a])

        stage = [tile("stage%d" % b, [P, 4 * W], F32) for b in range(2)]
        w1_c = [tile("w1_c%d" % b, [P, 1024], U32) for b in range(2)]
        w1_s = [tile("w1_s%d" % b, [P, 1024], U8) for b in range(2)]

        def quantise_w1(b):
            grouped = stage[b][:].bitcast(BF16).rearrange("p (t a m j) -> p a m j t", t=4, a=2, j=4)
            for a in range(2):
                nc.scalar.copy(grouped[:, a], w1_raw[b][a][:].rearrange("p j (m t) -> p m j t", t=4))
            nc.vector.quantize_mx(w1_c[b][:].bitcast(E4M3), w1_s[b][:], stage[b][:].bitcast(BF16))

        quantise_w1(0)
        quantise_w1(1)

        xb = [tile("xb0", [P, 2, 4, W], BF16), None]

        def read_page(c, s, buf):
            nc.vector.tensor_copy(buf, pages[s][:].indirect(list5[:, 32 * c : 32 * (c + 1)]))

        def apply_cap(c, s, buf):
            b, t = divmod(s, 4)
            nc.vector.tensor_scalar(xb[c][:, b, t, :], buf, cap_sb[:, b, t : t + 1], None, ALU.min)

        def quarter(i, k):
            return stage[i][:, W * k : W * (k + 1)]

        wa_c = tile("wa_c", [P, 2 * N], U32)
        wa_s = tile("wa_s", [P, 2 * N], U8)

        def quantise_wa():
            grouped = stage[0][:].bitcast(BF16).rearrange("p (a c i j) -> p a c j i", a=2, i=4, j=4)
            for a in range(2):
                nc.scalar.copy(grouped[:, a], wa_raw[a][:].rearrange("p j (c i) -> p c j i", i=4))
            nc.vector.quantize_mx(wa_c[:].bitcast(E4M3), wa_s[:], stage[0][:].bitcast(BF16))

        x_c = [[tile("x_c%d%d" % (c, a), [P, W], U32, tag="x%d%d" % (c, a)) for a in range(2)] for c in range(2)]
        x_s = [[tile("x_s%d%d" % (c, a), [P, W], U8) for a in range(2)] for c in range(2)]
        woven = tile("woven", [P, 4 * W], BF16)

        def quantise_x(c, a, grouped):
            nc.scalar.copy(
                grouped.rearrange("p (c i t) -> p c t i", i=4, t=4),
                xb[c][:, a].rearrange("p t (c i) -> p c t i", i=4),
            )
            nc.vector.quantize_mx(x_c[c][a][:].bitcast(E4M3), x_s[c][a][:], grouped)

        def put_h1(s):
            b, t = divmod(s, 4)
            bank = banks[3 + (s + 2) % 3]
            for a in range(2):
                cols = slice(256 * t + P * a, 256 * t + P * (a + 1))
                nc.tensor.matmul_mx(
                    out=bank[:], lhsT=w1_c[b][:, cols].bitcast(E4M3), lhsT_scale=w1_s[b][:, cols],
                    rhs=v_c[a][:].bitcast(E4M3), rhs_scale=v_s[4 * a :, :], start=(a == 0), stop=(a == 1),
                )
            nc.scalar.activation(hbuf[s % 4][:], bank[:], ACT.Abs)
            nc.vector.tensor_tensor(pages[s][:].indirect(list3[:]), hbuf[s % 4][:], f1[t][:], ALU.mult)

        picked = [quarter(0, 0), quarter(0, 1)] + [quarter(1, s % 4) for s in range(5)] + [quarter(0, 0)]
        for s in range(8):
            put_h1(s)
            if s >= 1:
                read_page(0, s - 1, picked[s - 1])
            if s >= 2:
                apply_cap(0, s - 2, picked[s - 2])
        quantise_wa()
        quantise_x(0, 0, woven[:])
        read_page(0, 7, picked[7])
        apply_cap(0, 6, picked[6])
        apply_cap(0, 7, picked[7])
        half = stage[1][:, 0 : 2 * W].bitcast(BF16)
        quantise_x(0, 1, half)
        xb[1] = tile("xb1", [P, 2, 4, W], BF16, tag="t2")
        for s, buf in ((7, quarter(0, 1)), (4, quarter(0, 0)), (5, quarter(1, 0)), (6, quarter(1, 1))):
            read_page(1, s, buf)
            apply_cap(1, s, buf)
        quantise_x(1, 1, woven[:])
        for s in range(4):
            read_page(1, s, quarter(1, s % 2))
            apply_cap(1, s, quarter(1, s % 2))

        bounded = tile("bounded", [P, 4, W], F32, tag="r00")
        offset = tile("offset", [P, 4, W], F32, tag="r01")
        scores = [tile("scores%d" % c, [P, 4, W], F32, tag="r1%d" % c) for c in range(2)]

        def product(bank, c, n, codes, plane):
            order = (0, 1) if c == 0 else (1, 0)
            for a in order:
                nc.tensor.matmul_mx(
                    out=bank[:], lhsT=codes(a, n), lhsT_scale=plane(a, n),
                    rhs=x_c[c][a][:].bitcast(E4M3), rhs_scale=x_s[c][a][:], start=(a == order[0]), stop=(a == order[1]),
                )

        def multiply(c, n):
            ya, yc, yb = banks[n % 2], banks[2 + n % 2], banks[4 + n]
            product(ya, c, n, lambda a, n: wa_c[:, N * a + P * n : N * a + P * (n + 1)].bitcast(E4M3),
                    lambda a, n: wa_s[:, N * a + P * n : N * a + P * (n + 1)])
            product(yb, c, n, lambda a, n: wb_w[:, a, P * n : P * (n + 1)].bitcast(E4M3),
                    lambda a, n: wb_plane[4 * a :, P * n : P * (n + 1)])
            product(yc, c, n, lambda a, n: wc_w[:, a, 256 * n : 256 * (n + 1)].bitcast(E2M1),
                    lambda a, n: wc_plane[:, N * a + P * n : N * a + P * (n + 1)])
            nc.scalar.activation(bounded[:, n, :], ya[:], ACT.Tanh)
            if c == 0:
                nc.scalar.copy(offset[:, n, :], yc[:])

        def score(c, n):
            larger = woven_last[:, W * (n - 2) : W * (n - 1)] if c == 0 and n >= 2 else quarter(1, n % 2)
            nc.vector.tensor_tensor(larger, bounded[:, n, :], banks[4 + n][:], ALU.max)
            taken = offset[:, n, :] if c == 0 else banks[2 + n % 2][:]
            pieces = 2 if (c, n) == (1, 3) else 1
            for i in range(pieces):
                cols = slice(W // pieces * i, W // pieces * (i + 1))
                nc.vector.tensor_tensor(scores[c][:, n, cols], larger[:, cols], taken[:, cols], ALU.subtract)
                nc.sync.dma_start(
                    out[P * n : P * (n + 1), W * c + cols.start : W * c + cols.stop], scores[c][:, n, cols]
                )

        for n in range(4):
            multiply(0, n)
        woven_last = tile("woven_last", [P, 2 * W], F32, tag="x00")
        quantise_x(1, 0, woven_last[:].bitcast(BF16))
        for n in range(4):
            score(0, n)
        for n in range(4):
            multiply(1, n)
            score(1, n)
